import numpy as np
import ml_dtypes

BF16 = ml_dtypes.bfloat16


def bf(x):
    return np.asarray(x, np.float32).astype(BF16)


def f32(x):
    return np.asarray(x, np.float32)


def f64(x):
    return np.asarray(x).astype(np.float64)


def striped(idx):
    return np.tile(idx.reshape(-1, 16).T, (8, 1))


S, A, K, M, N, E, Q = 256, 256, 128, 128, 192, 2, 96


def setup_inputs():
    return {"x": bf(np.random.standard_normal((A, S))), "wd": bf(np.random.standard_normal((A, M)) / np.sqrt(A)), "y": bf(np.random.standard_normal((K, N))), "w": bf(np.random.standard_normal((E, K, M)) / np.sqrt(K)), "b": f32(0.5 * np.random.standard_normal((M, 1))), "offs": striped(np.random.permutation(S)[:N])}


def reference(x, wd, y, w, b, offs):
    idx = offs[:16].T.reshape(-1)
    z = f64(wd).T @ f64(x)
    for e in range(E):
        z[:, idx[e * Q : (e + 1) * Q]] += f64(w)[e].T @ f64(y)[:, e * Q : (e + 1) * Q]
    return z + f64(b)

@@ -1,0 +1,64 @@
+import concourse.mybir as mybir
+
+BF16 = mybir.dt.bfloat16
+F32 = mybir.dt.float32
+U16 = mybir.dt.uint16
+
+P = 128
+FEATURES = 256
+TOKENS = 256
+EXPERTS = 2
+ENTRIES = 192
+PIECE = ENTRIES // EXPERTS
+OFFSETS_PER_COLUMN = 16
+
+FLOPS = 2 * FEATURES * P * TOKENS + 2 * P * P * ENTRIES
+
+
+def tile_rows_fillproj_bias_kernel(tc, x, wd, y, w, b, offs, out):
+    nc = tc.nc
+    blocks = FEATURES // P
+    with (
+        tc.tile_pool(name="held", bufs=1) as held,
+        tc.psum_pool(name="banks", bufs=1) as banks,
+    ):
+        x_tile = held.tile([P, blocks * TOKENS], BF16)
+        wd_tile = held.tile([P, blocks * P], BF16)
+        w_tile = held.tile([P, EXPERTS * P], BF16)
+        y_tile = held.tile([P, ENTRIES], BF16)
+        offsets = held.tile([P, ENTRIES // OFFSETS_PER_COLUMN], U16)
+        b_tile = held.tile([P, 1], F32)
+        out_tile = held.tile([P, TOKENS], F32)
+        window = banks.tile([P, TOKENS], F32)
+
+        nc.sync.dma_start(x_tile[:], x.rearrange("(p t) s -> p (t s)", t=blocks))
+        nc.sync.dma_start(wd_tile[:], wd.rearrange("(p t) m -> p (t m)", t=blocks))
+        nc.sync.dma_start(
+            w_tile[:].rearrange("k (e m) -> k e m", e=EXPERTS),
+            w.rearrange("e k m -> k e m"),
+        )
+        nc.sync.dma_start(y_tile[:], y)
+        nc.sync.dma_start(offsets[:], offs)
+        nc.scalar.dma_start(b_tile[:], b)
+
+        for t in range(blocks):
+            nc.tensor.matmul(
+                window[:],
+                wd_tile[:, t * P : (t + 1) * P],
+                x_tile[:, t * TOKENS : (t + 1) * TOKENS],
+                start=(t == 0),
+                stop=False,
+            )
+
+        columns = PIECE // OFFSETS_PER_COLUMN
+        for e in range(EXPERTS):
+            nc.tensor.matmul(
+                window[:].indirect(offsets[:, e * columns : (e + 1) * columns]),
+                w_tile[:, e * P : (e + 1) * P],
+                y_tile[:, e * PIECE : (e + 1) * PIECE],
+                start=False,
+                stop=(e == EXPERTS - 1),
+            )
+
+        nc.vector.tensor_scalar_add(out_tile[:], window[:], b_tile[:])
+        nc.sync.dma_start(out, out_tile[:])

@@ -11,6 +11,8 @@ EXPERTS = 2
 ENTRIES = 192
 PIECE = ENTRIES // EXPERTS
 OFFSETS_PER_COLUMN = 16
+WARM_COLUMNS = 512
+WARM_MATMULS = 4
 
 FLOPS = 2 * FEATURES * P * TOKENS + 2 * P * P * ENTRIES
 
@@ -30,6 +32,12 @@ def tile_rows_fillproj_bias_kernel(tc, x, wd, y, w, b, offs, out):
         b_tile = held.tile([P, 1], F32)
         out_tile = held.tile([P, TOKENS], F32)
         window = banks.tile([P, TOKENS], F32)
+
+        zeros = held.tile([P, WARM_COLUMNS], BF16)
+        warm_bank = banks.tile([P, WARM_COLUMNS], F32)
+        nc.vector.memset(zeros[:], 0.0)
+        for i in range(WARM_MATMULS):
+            nc.tensor.matmul(warm_bank[:], zeros[:, :P], zeros[:], start=True, stop=True)
 
         nc.sync.dma_start(x_tile[:], x.rearrange("(p t) s -> p (t s)", t=blocks))
         nc.sync.dma_start(wd_tile[:], wd.rearrange("(p t) m -> p (t m)", t=blocks))

@@ -11,8 +11,8 @@ EXPERTS = 2
 ENTRIES = 192
 PIECE = ENTRIES // EXPERTS
 OFFSETS_PER_COLUMN = 16
-WARM_COLUMNS = 512
-WARM_MATMULS = 4
+WARM_COLUMNS = 256
+WARM_MATMULS = 6
 
 FLOPS = 2 * FEATURES * P * TOKENS + 2 * P * P * ENTRIES
 
@@ -47,7 +47,7 @@ def tile_rows_fillproj_bias_kernel(tc, x, wd, y, w, b, offs, out):
         )
         nc.sync.dma_start(y_tile[:], y)
         nc.sync.dma_start(offsets[:], offs)
-        nc.scalar.dma_start(b_tile[:], b)
+        nc.sync.dma_start(b_tile[:], b)
 
         for t in range(blocks):
             nc.tensor.matmul(

@@ -40,8 +40,8 @@ def tile_rows_fillproj_bias_kernel(tc, x, wd, y, w, b, offs, out):
             nc.tensor.matmul(warm_bank[:], zeros[:, :P], zeros[:], start=True, stop=True)
 
         nc.sync.dma_start(x_tile[:], x.rearrange("(p t) s -> p (t s)", t=blocks))
-        nc.sync.dma_start(wd_tile[:], wd.rearrange("(p t) m -> p (t m)", t=blocks))
-        nc.sync.dma_start(
+        nc.scalar.dma_start(wd_tile[:], wd.rearrange("(p t) m -> p (t m)", t=blocks))
+        nc.scalar.dma_start(
             w_tile[:].rearrange("k (e m) -> k e m", e=EXPERTS),
             w.rearrange("e k m -> k e m"),
         )

import concourse.mybir as mybir

BF16 = mybir.dt.bfloat16
F32 = mybir.dt.float32
U16 = mybir.dt.uint16

P = 128
FEATURES = 256
TOKENS = 256
EXPERTS = 2
ENTRIES = 192
PIECE = ENTRIES // EXPERTS
OFFSETS_PER_COLUMN = 16
WARM_COLUMNS = 256
WARM_MATMULS = 6

FLOPS = 2 * FEATURES * P * TOKENS + 2 * P * P * ENTRIES


def tile_rows_fillproj_bias_kernel(tc, x, wd, y, w, b, offs, out):
    nc = tc.nc
    blocks = FEATURES // P
    with (
        tc.tile_pool(name="held", bufs=1) as held,
        tc.psum_pool(name="banks", bufs=1) as banks,
    ):
        x_tile = held.tile([P, blocks * TOKENS], BF16)
        wd_tile = held.tile([P, blocks * P], BF16)
        w_tile = held.tile([P, EXPERTS * P], BF16)
        y_tile = held.tile([P, ENTRIES], BF16)
        offsets = held.tile([P, ENTRIES // OFFSETS_PER_COLUMN], U16)
        b_tile = held.tile([P, 1], F32)
        out_tile = held.tile([P, TOKENS], F32)
        window = banks.tile([P, TOKENS], F32)

        zeros = held.tile([P, WARM_COLUMNS], BF16)
        warm_bank = banks.tile([P, WARM_COLUMNS], F32)
        nc.vector.memset(zeros[:], 0.0)
        for i in range(WARM_MATMULS):
            nc.tensor.matmul(warm_bank[:], zeros[:, :P], zeros[:], start=True, stop=True)

        nc.sync.dma_start(x_tile[:], x.rearrange("(p t) s -> p (t s)", t=blocks))
        nc.scalar.dma_start(wd_tile[:], wd.rearrange("(p t) m -> p (t m)", t=blocks))
        nc.scalar.dma_start(
            w_tile[:].rearrange("k (e m) -> k e m", e=EXPERTS),
            w.rearrange("e k m -> k e m"),
        )
        nc.sync.dma_start(y_tile[:], y)
        nc.sync.dma_start(offsets[:], offs)
        nc.sync.dma_start(b_tile[:], b)

        for t in range(blocks):
            nc.tensor.matmul(
                window[:],
                wd_tile[:, t * P : (t + 1) * P],
                x_tile[:, t * TOKENS : (t + 1) * TOKENS],
                start=(t == 0),
                stop=False,
            )

        columns = PIECE // OFFSETS_PER_COLUMN
        for e in range(EXPERTS):
            nc.tensor.matmul(
                window[:].indirect(offsets[:, e * columns : (e + 1) * columns]),
                w_tile[:, e * P : (e + 1) * P],
                y_tile[:, e * PIECE : (e + 1) * PIECE],
                start=False,
                stop=(e == EXPERTS - 1),
            )

        nc.vector.tensor_scalar_add(out_tile[:], window[:], b_tile[:])
        nc.sync.dma_start(out, out_tile[:])
